import numpy as np
import ml_dtypes


def mxq(x, axis, fmt="e4m3"):
    dtype, down = {"e4m3": (ml_dtypes.float8_e4m3fn, 7), "e5m2": (ml_dtypes.float8_e5m2, 14)}[fmt]
    v = np.moveaxis(np.asarray(x, np.float32).astype(ml_dtypes.bfloat16).astype(np.float64), axis, -1)
    blocks = v.reshape(v.shape[:-1] + (-1, 32))
    amax = np.abs(blocks).max(-1, keepdims=True)
    byte = np.maximum(np.where(amax > 0, np.frexp(amax)[1] - 1 + 127, 0) - down, 1)
    scale = np.exp2(byte - 127.0)
    codes = (blocks / scale).astype(np.float32).astype(dtype).astype(np.float64)
    return np.moveaxis((codes * scale).reshape(v.shape), -1, axis)


WIDE = False


def mx_kscale(k):
    if not WIDE:
        return np.ones(k)
    levels = np.array([10, -10, 5, -5, 0])
    if k % 512:
        return np.exp2(np.random.permutation(np.resize(levels, k // 32))).repeat(32)
    a = np.empty((k // 512, 16))
    for p in range(k // 512):
        a[p, :8] = np.random.permutation(np.resize(levels, 8))
        for g in range(8):
            far = levels[np.abs(levels - a[p, g]) >= 10]
            a[p, g + 8] = far[np.random.randint(len(far))]
    return np.exp2(a.ravel()).repeat(32)


def f64(x):
    return np.asarray(x).astype(np.float64)


def striped(idx):
    return np.tile(idx.reshape(-1, 16).T, (8, 1)).astype(np.uint16)


def unstriped(offs):
    return offs[:16].T.reshape(-1).astype(np.int64)


def pack_weight(w):
    k, n = w.shape
    w = f64(np.asarray(w, np.float32).astype(ml_dtypes.bfloat16)).reshape(k // 32, 32, n)
    amax = np.abs(w).max(1)
    byte = np.clip(np.where(amax > 0, np.frexp(amax)[1] - 1 + 127 - 7, 1), 1, 254)
    scaled = (w * np.exp2(127.0 - byte)[:, None, :]).reshape(k, n).astype(np.float32)
    words = np.ascontiguousarray(scaled.reshape(k // 512, 128, 4, n).transpose(0, 1, 3, 2)).astype(ml_dtypes.float8_e4m3fn).view(np.uint8)
    return words, np.ascontiguousarray(byte.astype(np.uint8).reshape(k // 512, 16, n))


def unpack_weight(words, scales):
    g, p, n, _ = words.shape
    vals = np.ascontiguousarray(words).view(ml_dtypes.float8_e4m3fn).astype(np.float64) * np.repeat(np.exp2(scales.astype(np.float64) - 127.0), 8, axis=1)[..., None]
    return vals.transpose(0, 1, 3, 2).reshape(g * 512, n)


E2M1 = np.array([0.0, 0.5, 1.0, 1.5, 2.0, 3.0, 4.0, 6.0, -0.0, -0.5, -1.0, -1.5, -2.0, -3.0, -4.0, -6.0])


def pack_fp4(w):
    k, n = w.shape
    w = f64(np.asarray(w, np.float32).astype(ml_dtypes.bfloat16)).reshape(k // 32, 32, n)
    amax = np.abs(w).max(1)
    mant, ex = np.frexp(amax / 6.0)
    byte = np.clip(np.where(amax > 0, np.where(mant > 0.5, ex, ex - 1) + 127, 1), 1, 254)
    scaled = (w * np.exp2(127.0 - byte)[:, None, :]).reshape(k, n).astype(np.float32)
    c = np.ascontiguousarray(scaled.reshape(k // 512, 128, 4, n).transpose(0, 1, 3, 2)).astype(ml_dtypes.float4_e2m1fn).view(np.uint8) & 0xF
    words = (c[..., 0::2] | (c[..., 1::2] << 4)).reshape(k // 512, 128, 2 * n)
    return np.ascontiguousarray(words), np.ascontiguousarray(byte.astype(np.uint8).reshape(k // 512, 16, n))


def unpack_fp4(words, scales):
    g, _, n = scales.shape
    words = np.ascontiguousarray(words).reshape(g, 128, n, 2)
    nib = np.empty((g, 128, n, 4), np.uint8)
    nib[..., 0::2] = words & 0xF
    nib[..., 1::2] = words >> 4
    vals = E2M1[nib] * np.repeat(np.exp2(scales.astype(np.float64) - 127.0), 8, axis=1)[..., None]
    return vals.transpose(0, 1, 3, 2).reshape(g * 512, n)


def planes(y):
    n, m = y.shape
    v = y.astype(np.float32).astype(ml_dtypes.bfloat16).astype(np.float64).reshape(n // 32, 32, m)
    top = np.abs(v).max(1)
    byte = np.clip(np.where(top > 0, np.frexp(top)[1] - 1 + 127 - 7, 1), 1, 254)
    codes = (v * np.exp2(127.0 - byte)[:, None, :]).reshape(n, m).astype(np.float32).astype(ml_dtypes.float8_e4m3fn).view(np.uint8)
    words = codes.reshape(n // 512, 128, 4, m).transpose(0, 1, 3, 2)
    return np.ascontiguousarray(words), np.ascontiguousarray(byte.astype(np.uint8).reshape(n // 512, 16, m))


K, T, S, N, H, U = 512, 2048, 512, 512, 512, 1024


def setup_inputs():
    n = np.random.standard_normal
    s = mx_kscale(K)[:, None]
    u = mx_kscale(H)
    packed_xT = pack_weight(n((K, T)) * s)
    packed_w1 = pack_fp4(n((K, N)) / np.sqrt(K) / s)
    packed_w2 = pack_fp4(n((K, N)) / np.sqrt(K) / s)
    packed_w3 = pack_fp4(n((H, N)) / np.sqrt(H) / u[:, None])
    return {
        "x_words": packed_xT[0],
        "x_scales": packed_xT[1],
        "w1_words": packed_w1[0],
        "w1_scales": packed_w1[1],
        "w2_words": packed_w2[0],
        "w2_scales": packed_w2[1],
        "unit": (np.random.uniform(0.6, 1.4, (H, 1)) * u[:, None]).astype(np.float32),
        "w3_words": packed_w3[0],
        "w3_scales": packed_w3[1],
        "offs": striped(np.random.permutation(T)[:S]),
        "snd": striped(np.random.permutation(np.concatenate([np.arange(S), np.random.randint(0, S, U - S)]))),
        "oth": striped(np.random.permutation(np.concatenate([np.arange(S), np.random.randint(0, S, U - S)]))),
    }


def reference(x_words, x_scales, w1_words, w1_scales, w2_words, w2_scales, unit, w3_words, w3_scales, offs, snd, oth):
    xq = unpack_weight(x_words, x_scales)[:, unstriped(offs)]
    y = unpack_fp4(w1_words, w1_scales).T @ xq
    ys = y[:, unstriped(snd)]
    yo = y[:, unstriped(oth)]
    dlt = ys - yo
    z1 = unpack_fp4(w2_words, w2_scales).T @ xq
    zs = z1[:, unstriped(snd)]
    zo = z1[:, unstriped(oth)]
    hid = f64(unit) * (np.minimum(np.maximum(dlt, zs), zo))
    out_0 = unpack_fp4(w3_words, w3_scales).T @ mxq(hid, 0, "e4m3")
    return (out_0,) + planes(out_0)

@@ -1,0 +1,206 @@
+from contextlib import ExitStack
+
+import concourse.mybir as mybir
+
+K, T, S, N, H, U = 512, 2048, 512, 512, 512, 1024
+FLOPS = 2 * K * N * S * 2 + 2 * H * N * U
+
+F32 = mybir.dt.float32
+BF16 = mybir.dt.bfloat16
+I32 = mybir.dt.int32
+U32 = mybir.dt.uint32
+U16 = mybir.dt.uint16
+U8 = mybir.dt.uint8
+FP8X4 = mybir.dt.float8_e4m3fn_x4
+FP4X4 = mybir.dt.float4_e2m1fn_x4
+ALU = mybir.AluOpType
+ACT = mybir.ActivationFunctionType
+
+P = 128
+PACK = 4
+QUADS = 4
+BANK = 512
+LIST_ROWS = 16
+Y_WINDOW = 2 * S
+Z_WINDOW = S + 16
+CHUNKS = (256, 256, 256, 128, 128)
+RUN = 4
+V_SENDER = ((0, 0), (0, 1), (0, 2), (0, 3))
+V_OTHER = ((0, 0), (0, 1))
+
+
+def load_scale_rows(queue, plane, rows):
+    for q in range(QUADS):
+        queue.dma_start(out=plane[32 * q : 32 * q + 4, :].bitcast(I32), in_=rows[0, 4 * q : 4 * q + 4, :].bitcast(I32))
+
+
+def deal_words(nc, dealt, raw):
+    nc.vector.tensor_copy(
+        out=dealt[:].rearrange("p (t m b) -> p t m b", t=PACK, b=2),
+        in_=raw[:].rearrange("p (m t b) -> p t m b", t=PACK, b=2),
+    )
+
+
+def deal_scales(nc, dealt, raw):
+    nc.vector.tensor_copy(
+        out=dealt[:].rearrange("p (t m) -> p t m", t=PACK),
+        in_=raw[:].rearrange("p (m t) -> p t m", t=PACK),
+    )
+
+
+def by_rows(ap):
+    return ap.rearrange("p t (c i) -> p c t i", i=RUN)
+
+
+def by_words(ap):
+    return ap.rearrange("p (c i t) -> p c t i", i=RUN, t=PACK)
+
+
+def tile_picked_ydiffex_clip_po_kernel(
+    tc, x_words, x_scales, w1_words, w1_scales, w2_words, w2_scales, unit, w3_words, w3_scales, offs, snd, oth, out_0, out_1, out_2
+):
+    nc = tc.nc
+    with ExitStack() as ctx:
+        keep = ctx.enter_context(tc.tile_pool(name="keep", bufs=1))
+        psum = ctx.enter_context(tc.psum_pool(name="psum", bufs=8))
+
+        offs_sb = keep.tile([P, S // LIST_ROWS], U16)
+        snd_sb = keep.tile([P, U // LIST_ROWS], U16)
+        oth_sb = keep.tile([P, U // LIST_ROWS], U16)
+        xw_all = keep.tile([P, T], I32, align_bytes=64)
+        xs_all = keep.tile([P, T], U8, align_bytes=64)
+        unit_sb = keep.tile([P, PACK], F32)
+        raw_w = [keep.tile([P, 2 * N], U8, name=f"raw_w{j}", align_bytes=64) for j in range(3)]
+        raw_s = [keep.tile([P, N], U8, name=f"raw_s{j}", align_bytes=64) for j in range(3)]
+        w_words = [keep.tile([P, 2 * N], U8, name=f"w_words{j}", align_bytes=64) for j in range(3)]
+        w_scales = [keep.tile([P, N], U8, name=f"w_scales{j}", align_bytes=64) for j in range(3)]
+        y_win = [keep.tile([P, Y_WINDOW], F32, name=f"y_win{t}", align_bytes=64) for t in range(PACK)]
+        z_win = [keep.tile([P, Z_WINDOW], F32, name=f"z_win{t}", align_bytes=64) for t in range(PACK)]
+
+        nc.vector.memset(xs_all[:].bitcast(I32), 0)
+        for j in range(3):
+            nc.vector.memset(raw_s[j][:].bitcast(I32), 0)
+
+        load_scale_rows(nc.gpsimd, raw_s[0], w1_scales)
+        nc.sync.dma_start(offs_sb[:], offs)
+        nc.scalar.dma_start(out=unit_sb[:], in_=unit.rearrange("(p t) o -> p (t o)", t=PACK))
+        load_scale_rows(nc.scalar, xs_all, x_scales)
+        nc.sync.dma_start(out=raw_w[0][:].bitcast(I32), in_=w1_words[0].bitcast(I32))
+        nc.sync.dma_start(out=xw_all[:], in_=x_words[0].rearrange("p c r -> p (c r)").bitcast(I32))
+        load_scale_rows(nc.sync, raw_s[1], w2_scales)
+        nc.sync.dma_start(out=raw_w[1][:].bitcast(I32), in_=w2_words[0].bitcast(I32))
+        nc.sync.dma_start(oth_sb[:], oth)
+        nc.sync.dma_start(snd_sb[:], snd)
+        nc.sync.dma_start(out=raw_w[2][:].bitcast(I32), in_=w3_words[0].bitcast(I32))
+        load_scale_rows(nc.sync, raw_s[2], w3_scales)
+
+        for t in range(PACK):
+            nc.vector.memset(y_win[t][:, S:], 0.0)
+            nc.vector.memset(z_win[t][:, S:], 0.0)
+
+        unit_sign = keep.tile([P, PACK], BF16)
+        nc.scalar.activation(out=unit_sign[:], in_=unit_sb[:], func=ACT.Sign)
+        unit_abs = keep.tile([P, PACK], F32)
+        nc.scalar.activation(out=unit_abs[:], in_=unit_sb[:], func=ACT.Abs)
+
+        xs = keep.tile([P, S], U8, align_bytes=64)
+        xw = keep.tile([P, S], U32, align_bytes=64)
+        deal_words(nc, w_words[0], raw_w[0])
+        nc.vector.tensor_copy(xs[:], xs_all[:].indirect(offs_sb[:]))
+        nc.vector.tensor_copy(xw[:], xw_all[:].bitcast(U32).indirect(offs_sb[:]))
+        deal_scales(nc, w_scales[0], raw_s[0])
+        deal_words(nc, w_words[1], raw_w[1])
+        deal_scales(nc, w_scales[1], raw_s[1])
+
+        def product(bank, j, t, codes, scales):
+            nc.tensor.matmul_mx(
+                out=bank,
+                lhsT=w_words[j][:, 2 * P * t : 2 * P * (t + 1)].bitcast(FP4X4),
+                lhsT_scale=w_scales[j][:, P * t : P * (t + 1)],
+                rhs=codes.bitcast(FP8X4),
+                rhs_scale=scales,
+                start=True,
+                stop=True,
+            )
+
+        for t in range(PACK):
+            y_bank = psum.tile([P, BANK], F32, name="y_bank", tag="bank")
+            product(y_bank[:], 0, t, xw[:], xs[:])
+            nc.scalar.activation(out=y_win[t][:, :S], in_=y_bank[:], func=ACT.Copy, scale=unit_abs[:, t : t + 1])
+            z_bank = psum.tile([P, BANK], F32, name="z_bank", tag="bank")
+            product(z_bank[:], 1, t, xw[:], xs[:])
+            nc.vector.tensor_scalar(out=z_win[t][:, :S], in0=z_bank[:], scalar1=unit_abs[:, t : t + 1], scalar2=None, op0=ALU.mult)
+
+        deal_words(nc, w_words[2], raw_w[2])
+        deal_scales(nc, w_scales[2], raw_s[2])
+
+        out_rows = out_0.rearrange("(p t) r -> p t r", t=PACK)
+        out_words = out_1[0].rearrange("p c r -> p (c r)").bitcast(I32)
+        o_codes = keep.tile([P, U], U32, align_bytes=64)
+        o_scales = keep.tile([P, U], U8, align_bytes=64)
+
+        def hidden(c, r0, n):
+            cols = slice(r0 // LIST_ROWS, (r0 + n) // LIST_ROWS)
+            yo = keep.tile([P, PACK, n], F32, name=f"yo{r0}", tag=f"yo{c % 2}")
+            dlt = keep.tile([P, PACK, n], F32, name=f"dlt{r0}")
+            gates = keep.tile([P, 2, PACK, n], F32, name=f"gates{r0}", tag=f"gates_hid{c % 2}", align_bytes=64)
+            zs, zo = gates[:, 0], gates[:, 1]
+            upper = keep.tile([P, PACK, n], F32, name=f"upper{r0}")
+            for t in range(PACK):
+                nc.scalar.activation(out=yo[:, t, :], in_=y_win[t][:].indirect(oth_sb[:, cols]), func=ACT.Copy)
+                if (c, t) in V_SENDER:
+                    nc.vector.tensor_copy(zs[:, t, :], z_win[t][:].indirect(snd_sb[:, cols]))
+                else:
+                    nc.scalar.activation(out=zs[:, t, :], in_=z_win[t][:].indirect(snd_sb[:, cols]), func=ACT.Copy)
+                nc.vector.tensor_tensor(dlt[:, t, :], y_win[t][:].indirect(snd_sb[:, cols]), yo[:, t, :], ALU.subtract)
+                if (c, t) in V_OTHER:
+                    nc.vector.tensor_copy(zo[:, t, :], z_win[t][:].indirect(oth_sb[:, cols]))
+                else:
+                    nc.scalar.activation(out=zo[:, t, :], in_=z_win[t][:].indirect(oth_sb[:, cols]), func=ACT.Copy)
+                if t % 2 == 1:
+                    nc.vector.tensor_tensor(upper[:, t - 1 : t + 1, :], dlt[:, t - 1 : t + 1, :], zs[:, t - 1 : t + 1, :], ALU.max)
+            clipped = keep.tile([P, PACK * n], BF16, name=f"clipped{r0}", align_bytes=64)
+            nc.vector.tensor_tensor(by_words(clipped[:]), by_rows(upper[:]), by_rows(zo), ALU.min)
+            hid = keep.tile([P, PACK * n], BF16, name=f"hid{r0}", tag=f"gates_hid{c % 2}", align_bytes=64)
+            nc.vector.tensor_tensor(
+                hid[:].rearrange("p (c t) -> p c t", t=PACK),
+                clipped[:].rearrange("p (c t) -> p c t", t=PACK),
+                unit_sign[:].unsqueeze(1).to_broadcast([P, n, PACK]),
+                ALU.mult,
+            )
+            h_codes = keep.tile([P, n], U32, name=f"h_codes{r0}", align_bytes=64)
+            h_scales = keep.tile([P, n], U8, name=f"h_scales{r0}", align_bytes=64)
+            nc.vector.quantize_mx(out=h_codes[:].bitcast(FP8X4), scales=h_scales[:], in_=hid[:])
+            return h_codes, h_scales
+
+        def shards(r0, n, h_codes, h_scales):
+            result = keep.tile([P, PACK, n], F32, name=f"result{r0}")
+            per_bank = BANK // n
+            for t0 in range(0, PACK, per_bank):
+                o_bank = psum.tile([P, BANK], F32, name="o_bank", tag="bank")
+                for j in range(per_bank):
+                    product(o_bank[:, j * n : (j + 1) * n], 2, t0 + j, h_codes[:], h_scales[:])
+                nc.scalar.activation(
+                    out=result[:, t0 : t0 + per_bank, :].rearrange("p t r -> p (t r)"), in_=o_bank[:], func=ACT.Copy
+                )
+            nc.sync.dma_start(out=out_rows[:, :, r0 : r0 + n], in_=result[:])
+            rounded = keep.tile([P, PACK * n], BF16, name=f"rounded{r0}", align_bytes=64)
+            nc.vector.tensor_copy(by_words(rounded[:]), by_rows(result[:]))
+            nc.vector.quantize_mx(
+                out=o_codes[:, r0 : r0 + n].bitcast(FP8X4), scales=o_scales[:, r0 : r0 + n], in_=rounded[:]
+            )
+            nc.sync.dma_start(out=out_words[:, r0 : r0 + n], in_=o_codes[:, r0 : r0 + n].bitcast(I32))
+
+        r0 = 0
+        pending = None
+        for c, n in enumerate(CHUNKS):
+            made = hidden(c, r0, n)
+            if pending is not None:
+                shards(*pending)
+            pending = (r0, n) + made
+            r0 = r0 + n
+        shards(*pending)
+
+        for q in range(QUADS):
+            queue = nc.sync if q % 2 == 0 else nc.scalar
+            queue.dma_start(out=out_2[0, 4 * q : 4 * q + 4, :].bitcast(I32), in_=o_scales[32 * q : 32 * q + 4, :].bitcast(I32))

@@ -21,23 +21,24 @@ PACK = 4
 QUADS = 4
 BANK = 512
 LIST_ROWS = 16
-Y_WINDOW = 2 * S
+Y_WINDOW = S + 16
 Z_WINDOW = S + 16
-CHUNKS = (256, 256, 256, 128, 128)
+CHUNKS = (512, 384, 128)
+WIDTHS = (128, 256, 512)
 RUN = 4
-V_SENDER = ((0, 0), (0, 1), (0, 2), (0, 3))
-V_OTHER = ((0, 0), (0, 1))
+V_SENDER = ((0, 1), (0, 2), (0, 3))
+V_OTHER = ()
 
 
-def load_scale_rows(queue, plane, rows):
-    for q in range(QUADS):
+def load_scale_rows(queues, plane, rows):
+    for q, queue in enumerate(queues):
         queue.dma_start(out=plane[32 * q : 32 * q + 4, :].bitcast(I32), in_=rows[0, 4 * q : 4 * q + 4, :].bitcast(I32))
 
 
 def deal_words(nc, dealt, raw):
     nc.vector.tensor_copy(
-        out=dealt[:].rearrange("p (t m b) -> p t m b", t=PACK, b=2),
-        in_=raw[:].rearrange("p (m t b) -> p t m b", t=PACK, b=2),
+        out=dealt[:].bitcast(U16).rearrange("p (t m) -> p t m", t=PACK),
+        in_=raw[:].bitcast(U16).rearrange("p (m t) -> p t m", t=PACK),
     )
 
 
@@ -70,47 +71,52 @@ def tile_picked_ydiffex_clip_po_kernel(
         xw_all = keep.tile([P, T], I32, align_bytes=64)
         xs_all = keep.tile([P, T], U8, align_bytes=64)
         unit_sb = keep.tile([P, PACK], F32)
-        raw_w = [keep.tile([P, 2 * N], U8, name=f"raw_w{j}", align_bytes=64) for j in range(3)]
-        raw_s = [keep.tile([P, N], U8, name=f"raw_s{j}", align_bytes=64) for j in range(3)]
+        raw_w = keep.tile([P, 2 * N], U8, align_bytes=64)
+        raw_w2 = keep.tile([P, 2 * N], U8, align_bytes=64)
+        raw_s = [keep.tile([P, N], U8, name=f"raw_s{j}", tag=f"raw_s{j}", align_bytes=64) for j in range(2)]
         w_words = [keep.tile([P, 2 * N], U8, name=f"w_words{j}", align_bytes=64) for j in range(3)]
         w_scales = [keep.tile([P, N], U8, name=f"w_scales{j}", align_bytes=64) for j in range(3)]
         y_win = [keep.tile([P, Y_WINDOW], F32, name=f"y_win{t}", align_bytes=64) for t in range(PACK)]
         z_win = [keep.tile([P, Z_WINDOW], F32, name=f"z_win{t}", align_bytes=64) for t in range(PACK)]
 
         nc.vector.memset(xs_all[:].bitcast(I32), 0)
-        for j in range(3):
-            nc.vector.memset(raw_s[j][:].bitcast(I32), 0)
+        nc.gpsimd.memset(raw_s[0][:].bitcast(I32), 0)
+        nc.vector.memset(raw_s[1][:].bitcast(I32), 0)
 
-        load_scale_rows(nc.gpsimd, raw_s[0], w1_scales)
+        xs_rows = keep.tile([P, T], U8, align_bytes=64)
         nc.sync.dma_start(offs_sb[:], offs)
-        nc.scalar.dma_start(out=unit_sb[:], in_=unit.rearrange("(p t) o -> p (t o)", t=PACK))
-        load_scale_rows(nc.scalar, xs_all, x_scales)
-        nc.sync.dma_start(out=raw_w[0][:].bitcast(I32), in_=w1_words[0].bitcast(I32))
+        load_scale_rows((nc.sync,) * QUADS, xs_rows, x_scales)
+        nc.sync.dma_start(out=raw_w[:].bitcast(I32), in_=w1_words[0].bitcast(I32))
         nc.sync.dma_start(out=xw_all[:], in_=x_words[0].rearrange("p c r -> p (c r)").bitcast(I32))
-        load_scale_rows(nc.sync, raw_s[1], w2_scales)
-        nc.sync.dma_start(out=raw_w[1][:].bitcast(I32), in_=w2_words[0].bitcast(I32))
+        load_scale_rows((nc.sync, nc.sync, nc.gpsimd, nc.gpsimd), raw_s[0], w1_scales)
+        nc.sync.dma_start(out=unit_sb[:], in_=unit.rearrange("(p t) o -> p (t o)", t=PACK))
         nc.sync.dma_start(oth_sb[:], oth)
         nc.sync.dma_start(snd_sb[:], snd)
-        nc.sync.dma_start(out=raw_w[2][:].bitcast(I32), in_=w3_words[0].bitcast(I32))
-        load_scale_rows(nc.sync, raw_s[2], w3_scales)
+        for q in range(QUADS):
+            live = slice(32 * q, 32 * q + 4)
+            nc.vector.tensor_copy(xs_all[live, :].bitcast(I32), xs_rows[live, :].bitcast(I32))
 
-        for t in range(PACK):
-            nc.vector.memset(y_win[t][:, S:], 0.0)
-            nc.vector.memset(z_win[t][:, S:], 0.0)
+        nc.vector.memset(y_win[0][:, S:], 0.0)
+        for window in y_win[1:] + z_win:
+            nc.scalar.activation(out=window[:, S:], in_=y_win[0][:, S:], func=ACT.Copy)
 
         unit_sign = keep.tile([P, PACK], BF16)
         nc.scalar.activation(out=unit_sign[:], in_=unit_sb[:], func=ACT.Sign)
-        unit_abs = keep.tile([P, PACK], F32)
-        nc.scalar.activation(out=unit_abs[:], in_=unit_sb[:], func=ACT.Abs)
 
         xs = keep.tile([P, S], U8, align_bytes=64)
         xw = keep.tile([P, S], U32, align_bytes=64)
-        deal_words(nc, w_words[0], raw_w[0])
+        deal_words(nc, w_words[0], raw_w)
+        nc.sync.dma_start(out=raw_w2[:].bitcast(I32), in_=w2_words[0].bitcast(I32))
+        load_scale_rows((nc.sync,) * QUADS, raw_s[1], w2_scales)
         nc.vector.tensor_copy(xs[:], xs_all[:].indirect(offs_sb[:]))
         nc.vector.tensor_copy(xw[:], xw_all[:].bitcast(U32).indirect(offs_sb[:]))
         deal_scales(nc, w_scales[0], raw_s[0])
-        deal_words(nc, w_words[1], raw_w[1])
+        deal_words(nc, w_words[1], raw_w2)
         deal_scales(nc, w_scales[1], raw_s[1])
+        unit_abs = keep.tile([P, PACK], F32, tag="raw_s1", align_bytes=64)
+        nc.vector.scalar_tensor_tensor(unit_abs[:], unit_sb[:], -1.0, unit_sb[:], ALU.mult, ALU.max)
+        nc.sync.dma_start(out=raw_w2[:].bitcast(I32), in_=w3_words[0].bitcast(I32))
+        load_scale_rows((nc.sync,) * QUADS, raw_s[0], w3_scales)
 
         def product(bank, j, t, codes, scales):
             nc.tensor.matmul_mx(
@@ -123,16 +129,19 @@ def tile_picked_ydiffex_clip_po_kernel(
                 stop=True,
             )
 
-        for t in range(PACK):
-            y_bank = psum.tile([P, BANK], F32, name="y_bank", tag="bank")
-            product(y_bank[:], 0, t, xw[:], xs[:])
-            nc.scalar.activation(out=y_win[t][:, :S], in_=y_bank[:], func=ACT.Copy, scale=unit_abs[:, t : t + 1])
-            z_bank = psum.tile([P, BANK], F32, name="z_bank", tag="bank")
-            product(z_bank[:], 1, t, xw[:], xs[:])
-            nc.vector.tensor_scalar(out=z_win[t][:, :S], in0=z_bank[:], scalar1=unit_abs[:, t : t + 1], scalar2=None, op0=ALU.mult)
+        for j, windows in enumerate((y_win, z_win)):
+            for t in range(PACK):
+                bank = psum.tile([P, BANK], F32, name="bank", tag="bank")
+                product(bank[:], j, t, xw[:], xs[:])
+                if j == 0 and t % 2 == 0:
+                    nc.scalar.activation(out=windows[t][:, :S], in_=bank[:], func=ACT.Copy, scale=unit_abs[:, t : t + 1])
+                else:
+                    nc.vector.tensor_scalar(
+                        out=windows[t][:, :S], in0=bank[:], scalar1=unit_abs[:, t : t + 1], scalar2=None, op0=ALU.mult
+                    )
 
-        deal_words(nc, w_words[2], raw_w[2])
-        deal_scales(nc, w_scales[2], raw_s[2])
+        deal_words(nc, w_words[2], raw_w2)
+        deal_scales(nc, w_scales[2], raw_s[0])
 
         out_rows = out_0.rearrange("(p t) r -> p t r", t=PACK)
         out_words = out_1[0].rearrange("p c r -> p (c r)").bitcast(I32)
@@ -142,17 +151,17 @@ def tile_picked_ydiffex_clip_po_kernel(
         def hidden(c, r0, n):
             cols = slice(r0 // LIST_ROWS, (r0 + n) // LIST_ROWS)
             yo = keep.tile([P, PACK, n], F32, name=f"yo{r0}", tag=f"yo{c % 2}")
-            dlt = keep.tile([P, PACK, n], F32, name=f"dlt{r0}")
-            gates = keep.tile([P, 2, PACK, n], F32, name=f"gates{r0}", tag=f"gates_hid{c % 2}", align_bytes=64)
+            dlt = keep.tile([P, PACK, n], F32, name=f"dlt{r0}", tag="raw_s1", align_bytes=64)
+            gates = keep.tile([P, 2, PACK, n], F32, name=f"gates{r0}", tag=f"gates_codes{c % 2}", align_bytes=64)
             zs, zo = gates[:, 0], gates[:, 1]
             upper = keep.tile([P, PACK, n], F32, name=f"upper{r0}")
             for t in range(PACK):
-                nc.scalar.activation(out=yo[:, t, :], in_=y_win[t][:].indirect(oth_sb[:, cols]), func=ACT.Copy)
+                nc.scalar.activation(out=yo[:, t, :], in_=y_win[t][:].indirect(oth_sb[:, cols]), func=ACT.Copy, scale=-1.0)
                 if (c, t) in V_SENDER:
                     nc.vector.tensor_copy(zs[:, t, :], z_win[t][:].indirect(snd_sb[:, cols]))
                 else:
                     nc.scalar.activation(out=zs[:, t, :], in_=z_win[t][:].indirect(snd_sb[:, cols]), func=ACT.Copy)
-                nc.vector.tensor_tensor(dlt[:, t, :], y_win[t][:].indirect(snd_sb[:, cols]), yo[:, t, :], ALU.subtract)
+                nc.vector.tensor_tensor(dlt[:, t, :], y_win[t][:].indirect(snd_sb[:, cols]), yo[:, t, :], ALU.add)
                 if (c, t) in V_OTHER:
                     nc.vector.tensor_copy(zo[:, t, :], z_win[t][:].indirect(oth_sb[:, cols]))
                 else:
@@ -161,31 +170,37 @@ def tile_picked_ydiffex_clip_po_kernel(
                     nc.vector.tensor_tensor(upper[:, t - 1 : t + 1, :], dlt[:, t - 1 : t + 1, :], zs[:, t - 1 : t + 1, :], ALU.max)
             clipped = keep.tile([P, PACK * n], BF16, name=f"clipped{r0}", align_bytes=64)
             nc.vector.tensor_tensor(by_words(clipped[:]), by_rows(upper[:]), by_rows(zo), ALU.min)
-            hid = keep.tile([P, PACK * n], BF16, name=f"hid{r0}", tag=f"gates_hid{c % 2}", align_bytes=64)
+            hid = keep.tile([P, PACK * n], BF16, name=f"hid{r0}", tag=f"hid_rounded{c}", align_bytes=64)
             nc.vector.tensor_tensor(
                 hid[:].rearrange("p (c t) -> p c t", t=PACK),
                 clipped[:].rearrange("p (c t) -> p c t", t=PACK),
                 unit_sign[:].unsqueeze(1).to_broadcast([P, n, PACK]),
                 ALU.mult,
             )
-            h_codes = keep.tile([P, n], U32, name=f"h_codes{r0}", align_bytes=64)
+            h_codes = keep.tile([P, n], U32, name=f"h_codes{r0}", tag=f"gates_codes{c % 2}", align_bytes=64)
             h_scales = keep.tile([P, n], U8, name=f"h_scales{r0}", align_bytes=64)
             nc.vector.quantize_mx(out=h_codes[:].bitcast(FP8X4), scales=h_scales[:], in_=hid[:])
             return h_codes, h_scales
 
-        def shards(r0, n, h_codes, h_scales):
+        def shards(c, r0, n, h_codes, h_scales):
             result = keep.tile([P, PACK, n], F32, name=f"result{r0}")
-            per_bank = BANK // n
-            for t0 in range(0, PACK, per_bank):
+            rounded = keep.tile([P, PACK * n], BF16, name=f"rounded{r0}", tag=f"hid_rounded{c + 1}", align_bytes=64)
+            one_bank = PACK * n == BANK
+            flat = result[:].rearrange("p t r -> p (t r)")
+            for first in range(0, PACK * n, BANK):
                 o_bank = psum.tile([P, BANK], F32, name="o_bank", tag="bank")
-                for j in range(per_bank):
-                    product(o_bank[:, j * n : (j + 1) * n], 2, t0 + j, h_codes[:], h_scales[:])
-                nc.scalar.activation(
-                    out=result[:, t0 : t0 + per_bank, :].rearrange("p t r -> p (t r)"), in_=o_bank[:], func=ACT.Copy
-                )
+                at = first
+                while at < first + BANK:
+                    t, r = divmod(at, n)
+                    width = max(w for w in WIDTHS if w <= min(n - r, first + BANK - at))
+                    product(o_bank[:, at - first : at - first + width], 2, t, h_codes[:, r : r + width], h_scales[:, r : r + width])
+                    at = at + width
+                if one_bank:
+                    nc.vector.tensor_copy(by_words(rounded[:]), by_rows(o_bank[:].rearrange("p (t r) -> p t r", t=PACK)))
+                nc.scalar.activation(out=flat[:, first : first + BANK], in_=o_bank[:], func=ACT.Copy)
             nc.sync.dma_start(out=out_rows[:, :, r0 : r0 + n], in_=result[:])
-            rounded = keep.tile([P, PACK * n], BF16, name=f"rounded{r0}", align_bytes=64)
-            nc.vector.tensor_copy(by_words(rounded[:]), by_rows(result[:]))
+            if not one_bank:
+                nc.vector.tensor_copy(by_words(rounded[:]), by_rows(result[:]))
             nc.vector.quantize_mx(
                 out=o_codes[:, r0 : r0 + n].bitcast(FP8X4), scales=o_scales[:, r0 : r0 + n], in_=rounded[:]
             )
@@ -197,7 +212,7 @@ def tile_picked_ydiffex_clip_po_kernel(
             made = hidden(c, r0, n)
             if pending is not None:
                 shards(*pending)
-            pending = (r0, n) + made
+            pending = (c, r0, n) + made
             r0 = r0 + n
         shards(*pending)
 

@@ -25,7 +25,7 @@ Y_WINDOW = S + 16
 Z_WINDOW = S + 16
 CHUNKS = (512, 384, 128)
 WIDTHS = (128, 256, 512)
-RUN = 4
+RUN = 2
 V_SENDER = ((0, 1), (0, 2), (0, 3))
 V_OTHER = ()
 
@@ -133,7 +133,7 @@ def tile_picked_ydiffex_clip_po_kernel(
             for t in range(PACK):
                 bank = psum.tile([P, BANK], F32, name="bank", tag="bank")
                 product(bank[:], j, t, xw[:], xs[:])
-                if j == 0 and t % 2 == 0:
+                if j == 0 and t < 3:
                     nc.scalar.activation(out=windows[t][:, :S], in_=bank[:], func=ACT.Copy, scale=unit_abs[:, t : t + 1])
                 else:
                     nc.vector.tensor_scalar(

@@ -26,7 +26,8 @@ Z_WINDOW = S + 16
 CHUNKS = (512, 384, 128)
 WIDTHS = (128, 256, 512)
 RUN = 2
-V_SENDER = ((0, 1), (0, 2), (0, 3))
+V_SENDER = ((0, 2), (0, 3))
+SHARED_SENDER = (0, 1)
 V_OTHER = ()
 
 
@@ -129,11 +130,11 @@ def tile_picked_ydiffex_clip_po_kernel(
                 stop=True,
             )
 
-        for j, windows in enumerate((y_win, z_win)):
-            for t in range(PACK):
+        for t in range(PACK):
+            for j, windows in enumerate((y_win, z_win)):
                 bank = psum.tile([P, BANK], F32, name="bank", tag="bank")
                 product(bank[:], j, t, xw[:], xs[:])
-                if j == 0 and t < 3:
+                if j == 0 and t != 1:
                     nc.scalar.activation(out=windows[t][:, :S], in_=bank[:], func=ACT.Copy, scale=unit_abs[:, t : t + 1])
                 else:
                     nc.vector.tensor_scalar(
@@ -157,7 +158,11 @@ def tile_picked_ydiffex_clip_po_kernel(
             upper = keep.tile([P, PACK, n], F32, name=f"upper{r0}")
             for t in range(PACK):
                 nc.scalar.activation(out=yo[:, t, :], in_=y_win[t][:].indirect(oth_sb[:, cols]), func=ACT.Copy, scale=-1.0)
-                if (c, t) in V_SENDER:
+                if (c, t) == SHARED_SENDER:
+                    mid = (cols.start + cols.stop) // 2
+                    nc.vector.tensor_copy(zs[:, t, : n // 2], z_win[t][:].indirect(snd_sb[:, cols.start : mid]))
+                    nc.scalar.activation(out=zs[:, t, n // 2 :], in_=z_win[t][:].indirect(snd_sb[:, mid : cols.stop]), func=ACT.Copy)
+                elif (c, t) in V_SENDER:
                     nc.vector.tensor_copy(zs[:, t, :], z_win[t][:].indirect(snd_sb[:, cols]))
                 else:
                     nc.scalar.activation(out=zs[:, t, :], in_=z_win[t][:].indirect(snd_sb[:, cols]), func=ACT.Copy)
@@ -185,21 +190,26 @@ def tile_picked_ydiffex_clip_po_kernel(
         def shards(c, r0, n, h_codes, h_scales):
             result = keep.tile([P, PACK, n], F32, name=f"result{r0}")
             rounded = keep.tile([P, PACK * n], BF16, name=f"rounded{r0}", tag=f"hid_rounded{c + 1}", align_bytes=64)
-            one_bank = PACK * n == BANK
             flat = result[:].rearrange("p t r -> p (t r)")
-            for first in range(0, PACK * n, BANK):
-                o_bank = psum.tile([P, BANK], F32, name="o_bank", tag="bank")
-                at = first
-                while at < first + BANK:
-                    t, r = divmod(at, n)
-                    width = max(w for w in WIDTHS if w <= min(n - r, first + BANK - at))
-                    product(o_bank[:, at - first : at - first + width], 2, t, h_codes[:, r : r + width], h_scales[:, r : r + width])
-                    at = at + width
-                if one_bank:
-                    nc.vector.tensor_copy(by_words(rounded[:]), by_rows(o_bank[:].rearrange("p (t r) -> p t r", t=PACK)))
-                nc.scalar.activation(out=flat[:, first : first + BANK], in_=o_bank[:], func=ACT.Copy)
-            nc.sync.dma_start(out=out_rows[:, :, r0 : r0 + n], in_=result[:])
-            if not one_bank:
+            if c == len(CHUNKS) - 1:
+                banks = [psum.tile([P, 2, n], F32, name=f"pair_bank{h}", tag="bank") for h in range(2)]
+                for t in range(PACK):
+                    product(banks[t // 2][:, t % 2, :], 2, t, h_codes[:], h_scales[:])
+                for h in range(2):
+                    nc.vector.tensor_copy(by_words(rounded[:])[:, :, 2 * h : 2 * h + 2, :], by_rows(banks[h][:]))
+                    nc.scalar.activation(out=result[:, 2 - 2 * h : 4 - 2 * h, :], in_=banks[1 - h][:], func=ACT.Copy)
+                nc.sync.dma_start(out=out_rows[:, :, r0 : r0 + n], in_=result[:])
+            else:
+                for first in range(0, PACK * n, BANK):
+                    o_bank = psum.tile([P, BANK], F32, name="o_bank", tag="bank")
+                    at = first
+                    while at < first + BANK:
+                        t, r = divmod(at, n)
+                        width = max(w for w in WIDTHS if w <= min(n - r, first + BANK - at))
+                        product(o_bank[:, at - first : at - first + width], 2, t, h_codes[:, r : r + width], h_scales[:, r : r + width])
+                        at = at + width
+                    nc.scalar.activation(out=flat[:, first : first + BANK], in_=o_bank[:], func=ACT.Copy)
+                nc.sync.dma_start(out=out_rows[:, :, r0 : r0 + n], in_=result[:])
                 nc.vector.tensor_copy(by_words(rounded[:]), by_rows(result[:]))
             nc.vector.quantize_mx(
                 out=o_codes[:, r0 : r0 + n].bitcast(FP8X4), scales=o_scales[:, r0 : r0 + n], in_=rounded[:]

from contextlib import ExitStack

import concourse.mybir as mybir

K, T, S, N, H, U = 512, 2048, 512, 512, 512, 1024
FLOPS = 2 * K * N * S * 2 + 2 * H * N * U

F32 = mybir.dt.float32
BF16 = mybir.dt.bfloat16
I32 = mybir.dt.int32
U32 = mybir.dt.uint32
U16 = mybir.dt.uint16
U8 = mybir.dt.uint8
FP8X4 = mybir.dt.float8_e4m3fn_x4
FP4X4 = mybir.dt.float4_e2m1fn_x4
ALU = mybir.AluOpType
ACT = mybir.ActivationFunctionType

P = 128
PACK = 4
QUADS = 4
BANK = 512
LIST_ROWS = 16
Y_WINDOW = S + 16
Z_WINDOW = S + 16
CHUNKS = (512, 384, 128)
WIDTHS = (128, 256, 512)
RUN = 2
V_SENDER = ((0, 2), (0, 3))
SHARED_SENDER = (0, 1)
V_OTHER = ()


def load_scale_rows(queues, plane, rows):
    for q, queue in enumerate(queues):
        queue.dma_start(out=plane[32 * q : 32 * q + 4, :].bitcast(I32), in_=rows[0, 4 * q : 4 * q + 4, :].bitcast(I32))


def deal_words(nc, dealt, raw):
    nc.vector.tensor_copy(
        out=dealt[:].bitcast(U16).rearrange("p (t m) -> p t m", t=PACK),
        in_=raw[:].bitcast(U16).rearrange("p (m t) -> p t m", t=PACK),
    )


def deal_scales(nc, dealt, raw):
    nc.vector.tensor_copy(
        out=dealt[:].rearrange("p (t m) -> p t m", t=PACK),
        in_=raw[:].rearrange("p (m t) -> p t m", t=PACK),
    )


def by_rows(ap):
    return ap.rearrange("p t (c i) -> p c t i", i=RUN)


def by_words(ap):
    return ap.rearrange("p (c i t) -> p c t i", i=RUN, t=PACK)


def tile_picked_ydiffex_clip_po_kernel(
    tc, x_words, x_scales, w1_words, w1_scales, w2_words, w2_scales, unit, w3_words, w3_scales, offs, snd, oth, out_0, out_1, out_2
):
    nc = tc.nc
    with ExitStack() as ctx:
        keep = ctx.enter_context(tc.tile_pool(name="keep", bufs=1))
        psum = ctx.enter_context(tc.psum_pool(name="psum", bufs=8))

        offs_sb = keep.tile([P, S // LIST_ROWS], U16)
        snd_sb = keep.tile([P, U // LIST_ROWS], U16)
        oth_sb = keep.tile([P, U // LIST_ROWS], U16)
        xw_all = keep.tile([P, T], I32, align_bytes=64)
        xs_all = keep.tile([P, T], U8, align_bytes=64)
        unit_sb = keep.tile([P, PACK], F32)
        raw_w = keep.tile([P, 2 * N], U8, align_bytes=64)
        raw_w2 = keep.tile([P, 2 * N], U8, align_bytes=64)
        raw_s = [keep.tile([P, N], U8, name=f"raw_s{j}", tag=f"raw_s{j}", align_bytes=64) for j in range(2)]
        w_words = [keep.tile([P, 2 * N], U8, name=f"w_words{j}", align_bytes=64) for j in range(3)]
        w_scales = [keep.tile([P, N], U8, name=f"w_scales{j}", align_bytes=64) for j in range(3)]
        y_win = [keep.tile([P, Y_WINDOW], F32, name=f"y_win{t}", align_bytes=64) for t in range(PACK)]
        z_win = [keep.tile([P, Z_WINDOW], F32, name=f"z_win{t}", align_bytes=64) for t in range(PACK)]

        nc.vector.memset(xs_all[:].bitcast(I32), 0)
        nc.gpsimd.memset(raw_s[0][:].bitcast(I32), 0)
        nc.vector.memset(raw_s[1][:].bitcast(I32), 0)

        xs_rows = keep.tile([P, T], U8, align_bytes=64)
        nc.sync.dma_start(offs_sb[:], offs)
        load_scale_rows((nc.sync,) * QUADS, xs_rows, x_scales)
        nc.sync.dma_start(out=raw_w[:].bitcast(I32), in_=w1_words[0].bitcast(I32))
        nc.sync.dma_start(out=xw_all[:], in_=x_words[0].rearrange("p c r -> p (c r)").bitcast(I32))
        load_scale_rows((nc.sync, nc.sync, nc.gpsimd, nc.gpsimd), raw_s[0], w1_scales)
        nc.sync.dma_start(out=unit_sb[:], in_=unit.rearrange("(p t) o -> p (t o)", t=PACK))
        nc.sync.dma_start(oth_sb[:], oth)
        nc.sync.dma_start(snd_sb[:], snd)
        for q in range(QUADS):
            live = slice(32 * q, 32 * q + 4)
            nc.vector.tensor_copy(xs_all[live, :].bitcast(I32), xs_rows[live, :].bitcast(I32))

        nc.vector.memset(y_win[0][:, S:], 0.0)
        for window in y_win[1:] + z_win:
            nc.scalar.activation(out=window[:, S:], in_=y_win[0][:, S:], func=ACT.Copy)

        unit_sign = keep.tile([P, PACK], BF16)
        nc.scalar.activation(out=unit_sign[:], in_=unit_sb[:], func=ACT.Sign)

        xs = keep.tile([P, S], U8, align_bytes=64)
        xw = keep.tile([P, S], U32, align_bytes=64)
        deal_words(nc, w_words[0], raw_w)
        nc.sync.dma_start(out=raw_w2[:].bitcast(I32), in_=w2_words[0].bitcast(I32))
        load_scale_rows((nc.sync,) * QUADS, raw_s[1], w2_scales)
        nc.vector.tensor_copy(xs[:], xs_all[:].indirect(offs_sb[:]))
        nc.vector.tensor_copy(xw[:], xw_all[:].bitcast(U32).indirect(offs_sb[:]))
        deal_scales(nc, w_scales[0], raw_s[0])
        deal_words(nc, w_words[1], raw_w2)
        deal_scales(nc, w_scales[1], raw_s[1])
        unit_abs = keep.tile([P, PACK], F32, tag="raw_s1", align_bytes=64)
        nc.vector.scalar_tensor_tensor(unit_abs[:], unit_sb[:], -1.0, unit_sb[:], ALU.mult, ALU.max)
        nc.sync.dma_start(out=raw_w2[:].bitcast(I32), in_=w3_words[0].bitcast(I32))
        load_scale_rows((nc.sync,) * QUADS, raw_s[0], w3_scales)

        def product(bank, j, t, codes, scales):
            nc.tensor.matmul_mx(
                out=bank,
                lhsT=w_words[j][:, 2 * P * t : 2 * P * (t + 1)].bitcast(FP4X4),
                lhsT_scale=w_scales[j][:, P * t : P * (t + 1)],
                rhs=codes.bitcast(FP8X4),
                rhs_scale=scales,
                start=True,
                stop=True,
            )

        for t in range(PACK):
            for j, windows in enumerate((y_win, z_win)):
                bank = psum.tile([P, BANK], F32, name="bank", tag="bank")
                product(bank[:], j, t, xw[:], xs[:])
                if j == 0 and t != 1:
                    nc.scalar.activation(out=windows[t][:, :S], in_=bank[:], func=ACT.Copy, scale=unit_abs[:, t : t + 1])
                else:
                    nc.vector.tensor_scalar(
                        out=windows[t][:, :S], in0=bank[:], scalar1=unit_abs[:, t : t + 1], scalar2=None, op0=ALU.mult
                    )

        deal_words(nc, w_words[2], raw_w2)
        deal_scales(nc, w_scales[2], raw_s[0])

        out_rows = out_0.rearrange("(p t) r -> p t r", t=PACK)
        out_words = out_1[0].rearrange("p c r -> p (c r)").bitcast(I32)
        o_codes = keep.tile([P, U], U32, align_bytes=64)
        o_scales = keep.tile([P, U], U8, align_bytes=64)

        def hidden(c, r0, n):
            cols = slice(r0 // LIST_ROWS, (r0 + n) // LIST_ROWS)
            yo = keep.tile([P, PACK, n], F32, name=f"yo{r0}", tag=f"yo{c % 2}")
            dlt = keep.tile([P, PACK, n], F32, name=f"dlt{r0}", tag="raw_s1", align_bytes=64)
            gates = keep.tile([P, 2, PACK, n], F32, name=f"gates{r0}", tag=f"gates_codes{c % 2}", align_bytes=64)
            zs, zo = gates[:, 0], gates[:, 1]
            upper = keep.tile([P, PACK, n], F32, name=f"upper{r0}")
            for t in range(PACK):
                nc.scalar.activation(out=yo[:, t, :], in_=y_win[t][:].indirect(oth_sb[:, cols]), func=ACT.Copy, scale=-1.0)
                if (c, t) == SHARED_SENDER:
                    mid = (cols.start + cols.stop) // 2
                    nc.vector.tensor_copy(zs[:, t, : n // 2], z_win[t][:].indirect(snd_sb[:, cols.start : mid]))
                    nc.scalar.activation(out=zs[:, t, n // 2 :], in_=z_win[t][:].indirect(snd_sb[:, mid : cols.stop]), func=ACT.Copy)
                elif (c, t) in V_SENDER:
                    nc.vector.tensor_copy(zs[:, t, :], z_win[t][:].indirect(snd_sb[:, cols]))
                else:
                    nc.scalar.activation(out=zs[:, t, :], in_=z_win[t][:].indirect(snd_sb[:, cols]), func=ACT.Copy)
                nc.vector.tensor_tensor(dlt[:, t, :], y_win[t][:].indirect(snd_sb[:, cols]), yo[:, t, :], ALU.add)
                if (c, t) in V_OTHER:
                    nc.vector.tensor_copy(zo[:, t, :], z_win[t][:].indirect(oth_sb[:, cols]))
                else:
                    nc.scalar.activation(out=zo[:, t, :], in_=z_win[t][:].indirect(oth_sb[:, cols]), func=ACT.Copy)
                if t % 2 == 1:
                    nc.vector.tensor_tensor(upper[:, t - 1 : t + 1, :], dlt[:, t - 1 : t + 1, :], zs[:, t - 1 : t + 1, :], ALU.max)
            clipped = keep.tile([P, PACK * n], BF16, name=f"clipped{r0}", align_bytes=64)
            nc.vector.tensor_tensor(by_words(clipped[:]), by_rows(upper[:]), by_rows(zo), ALU.min)
            hid = keep.tile([P, PACK * n], BF16, name=f"hid{r0}", tag=f"hid_rounded{c}", align_bytes=64)
            nc.vector.tensor_tensor(
                hid[:].rearrange("p (c t) -> p c t", t=PACK),
                clipped[:].rearrange("p (c t) -> p c t", t=PACK),
                unit_sign[:].unsqueeze(1).to_broadcast([P, n, PACK]),
                ALU.mult,
            )
            h_codes = keep.tile([P, n], U32, name=f"h_codes{r0}", tag=f"gates_codes{c % 2}", align_bytes=64)
            h_scales = keep.tile([P, n], U8, name=f"h_scales{r0}", align_bytes=64)
            nc.vector.quantize_mx(out=h_codes[:].bitcast(FP8X4), scales=h_scales[:], in_=hid[:])
            return h_codes, h_scales

        def shards(c, r0, n, h_codes, h_scales):
            result = keep.tile([P, PACK, n], F32, name=f"result{r0}")
            rounded = keep.tile([P, PACK * n], BF16, name=f"rounded{r0}", tag=f"hid_rounded{c + 1}", align_bytes=64)
            flat = result[:].rearrange("p t r -> p (t r)")
            if c == len(CHUNKS) - 1:
                banks = [psum.tile([P, 2, n], F32, name=f"pair_bank{h}", tag="bank") for h in range(2)]
                for t in range(PACK):
                    product(banks[t // 2][:, t % 2, :], 2, t, h_codes[:], h_scales[:])
                for h in range(2):
                    nc.vector.tensor_copy(by_words(rounded[:])[:, :, 2 * h : 2 * h + 2, :], by_rows(banks[h][:]))
                    nc.scalar.activation(out=result[:, 2 - 2 * h : 4 - 2 * h, :], in_=banks[1 - h][:], func=ACT.Copy)
                nc.sync.dma_start(out=out_rows[:, :, r0 : r0 + n], in_=result[:])
            else:
                for first in range(0, PACK * n, BANK):
                    o_bank = psum.tile([P, BANK], F32, name="o_bank", tag="bank")
                    at = first
                    while at < first + BANK:
                        t, r = divmod(at, n)
                        width = max(w for w in WIDTHS if w <= min(n - r, first + BANK - at))
                        product(o_bank[:, at - first : at - first + width], 2, t, h_codes[:, r : r + width], h_scales[:, r : r + width])
                        at = at + width
                    nc.scalar.activation(out=flat[:, first : first + BANK], in_=o_bank[:], func=ACT.Copy)
                nc.sync.dma_start(out=out_rows[:, :, r0 : r0 + n], in_=result[:])
                nc.vector.tensor_copy(by_words(rounded[:]), by_rows(result[:]))
            nc.vector.quantize_mx(
                out=o_codes[:, r0 : r0 + n].bitcast(FP8X4), scales=o_scales[:, r0 : r0 + n], in_=rounded[:]
            )
            nc.sync.dma_start(out=out_words[:, r0 : r0 + n], in_=o_codes[:, r0 : r0 + n].bitcast(I32))

        r0 = 0
        pending = None
        for c, n in enumerate(CHUNKS):
            made = hidden(c, r0, n)
            if pending is not None:
                shards(*pending)
            pending = (c, r0, n) + made
            r0 = r0 + n
        shards(*pending)

        for q in range(QUADS):
            queue = nc.sync if q % 2 == 0 else nc.scalar
            queue.dma_start(out=out_2[0, 4 * q : 4 * q + 4, :].bitcast(I32), in_=o_scales[32 * q : 32 * q + 4, :].bitcast(I32))
